import numpy as np
import ml_dtypes


def mxq(x, axis, fmt="e4m3"):
    dtype, down = {"e4m3": (ml_dtypes.float8_e4m3fn, 7), "e5m2": (ml_dtypes.float8_e5m2, 14)}[fmt]
    v = np.moveaxis(np.asarray(x, np.float32).astype(ml_dtypes.bfloat16).astype(np.float64), axis, -1)
    blocks = v.reshape(v.shape[:-1] + (-1, 32))
    amax = np.abs(blocks).max(-1, keepdims=True)
    byte = np.maximum(np.where(amax > 0, np.frexp(amax)[1] - 1 + 127, 0) - down, 1)
    scale = np.exp2(byte - 127.0)
    codes = (blocks / scale).astype(np.float32).astype(dtype).astype(np.float64)
    return np.moveaxis((codes * scale).reshape(v.shape), -1, axis)


WIDE = False


def mx_kscale(k):
    if not WIDE:
        return np.ones(k)
    levels = np.array([10, -10, 5, -5, 0])
    if k % 512:
        return np.exp2(np.random.permutation(np.resize(levels, k // 32))).repeat(32)
    a = np.empty((k // 512, 16))
    for p in range(k // 512):
        a[p, :8] = np.random.permutation(np.resize(levels, 8))
        for g in range(8):
            far = levels[np.abs(levels - a[p, g]) >= 10]
            a[p, g + 8] = far[np.random.randint(len(far))]
    return np.exp2(a.ravel()).repeat(32)


def f64(x):
    return np.asarray(x).astype(np.float64)


def striped(idx):
    return np.tile(idx.reshape(-1, 16).T, (8, 1)).astype(np.uint16)


def unstriped(offs):
    return offs[:16].T.reshape(-1).astype(np.int64)


E2M1 = np.array([0.0, 0.5, 1.0, 1.5, 2.0, 3.0, 4.0, 6.0, -0.0, -0.5, -1.0, -1.5, -2.0, -3.0, -4.0, -6.0])


def pack_weight(w, fmt):
    k, n = w.shape
    w = f64(np.asarray(w, np.float32).astype(ml_dtypes.bfloat16)).reshape(k // 32, 32, n)
    amax = np.abs(w).max(1)
    if fmt == "e4m3":
        byte = np.frexp(amax)[1] - 1 + 127 - 7
    else:
        mant, ex = np.frexp(amax / 6.0)
        byte = np.where(mant > 0.5, ex, ex - 1) + 127
    byte = np.clip(np.where(amax > 0, byte, 1), 1, 254)
    scaled = (w * np.exp2(127.0 - byte)[:, None, :]).reshape(k, n).astype(np.float32)
    by_word = np.ascontiguousarray(scaled.reshape(k // 512, 128, 4, n).transpose(0, 1, 3, 2))
    if fmt == "e4m3":
        words = by_word.astype(ml_dtypes.float8_e4m3fn).view(np.uint8)
    else:
        c = by_word.astype(ml_dtypes.float4_e2m1fn).view(np.uint8) & 0xF
        words = (c[..., 0::2] | (c[..., 1::2] << 4)).reshape(k // 512, 128, 2 * n)
    return np.ascontiguousarray(words), np.ascontiguousarray(byte.astype(np.uint8).reshape(k // 512, 16, n))


def unpack_weight(words, scales, fmt):
    g, _, n = scales.shape
    words = np.ascontiguousarray(words).reshape(g, 128, n, -1)
    if fmt == "e4m3":
        vals = words.view(ml_dtypes.float8_e4m3fn).astype(np.float64)
    else:
        nib = np.empty((g, 128, n, 4), np.uint8)
        nib[..., 0::2] = words & 0xF
        nib[..., 1::2] = words >> 4
        vals = E2M1[nib]
    vals = vals * np.repeat(np.exp2(scales.astype(np.float64) - 127.0), 8, axis=1)[..., None]
    return vals.transpose(0, 1, 3, 2).reshape(g * 512, n)


def gelu(v):
    return 0.5 * v * (1.0 + np.tanh(np.sqrt(2.0 / np.pi) * (v + 0.044715 * v**3)))


K, H, M, N, T, S, T3, P = 1024, 1024, 512, 512, 4096, 1024, 2048, 512

def setup_inputs():
    n = np.random.standard_normal
    s = mx_kscale(K)[:, None]
    u = mx_kscale(H)[:, None]
    s2 = mx_kscale(M)[:, None]
    tab_words, tab_scales = pack_weight(n((K, T)) * s, "e4m3")
    tab2_words, tab2_scales = pack_weight(n((M, T3)) * s2, "e4m3")
    w4_words, w4_scales = pack_weight(1.3 * n((H, N)) / np.sqrt(H) / u, "e2m1")
    w8_words, w8_scales = pack_weight(n((M, N)) / np.sqrt(M) / s2, "e4m3")
    return {
        "tab_words": tab_words, "tab_scales": tab_scales,
        "offs": striped(np.random.permutation(T)[:S]),
        "w1": (1.1 * n((K, H)) / np.sqrt(K) / s).astype(np.float32),
        "stain": (0.9 * n((H, S))).astype(np.float32),
        "gain": (np.exp(0.3 * n(H)) * u[:, 0]).astype(np.float32),
        "w4_words": w4_words, "w4_scales": w4_scales,
        "tab2_words": tab2_words, "tab2_scales": tab2_scales,
        "offs2": striped(np.random.permutation(T3)[:P]),
        "w8_words": w8_words, "w8_scales": w8_scales,
        "pos1": striped(np.random.permutation(S)[:P]),
        "res": (0.8 * n((N, P))).astype(np.float32),
    }

def reference(tab_words, tab_scales, offs, w1, stain, gain, w4_words, w4_scales,
              tab2_words, tab2_scales, offs2, w8_words, w8_scales, pos1, res):
    v = unpack_weight(tab_words, tab_scales, "e4m3")[:, unstriped(offs)]
    v2 = unpack_weight(tab2_words, tab2_scales, "e4m3")[:, unstriped(offs2)]
    w4 = unpack_weight(w4_words, w4_scales, "e2m1")
    w8 = unpack_weight(w8_words, w8_scales, "e4m3")
    h = (mxq(f64(w1), 0, "e4m3").T @ v) + f64(stain)
    h = np.tanh(h) * f64(gain)[:, None]
    y = w4.T @ mxq(h, 0, "e4m3")
    b = w8.T @ v2
    return (y[:, unstriped(pos1)] + f64(res)) * b

@@ -1,0 +1,279 @@
+from contextlib import ExitStack
+
+import concourse.mybir as mybir
+
+K, H, M, N, T, S, T3, J = 1024, 1024, 512, 512, 4096, 1024, 2048, 512
+FLOPS = 2 * (K * H * S + H * N * S + M * N * J)
+
+F32 = mybir.dt.float32
+BF16 = mybir.dt.bfloat16
+I32 = mybir.dt.int32
+U32 = mybir.dt.uint32
+U16 = mybir.dt.uint16
+U8 = mybir.dt.uint8
+FP8X4 = mybir.dt.float8_e4m3fn_x4
+FP4X4 = mybir.dt.float4_e2m1fn_x4
+ADD = mybir.AluOpType.add
+MULT = mybir.AluOpType.mult
+TANH = mybir.ActivationFunctionType.Tanh
+
+P = 128
+PACK = 4
+PASS = P * PACK
+QUADS = 4
+COLS = 256
+LIST_ROWS = 16
+
+
+def tile_list_smear_strip_scores_kernel(
+    tc, tab_words, tab_scales, offs, w1, stain, gain, w4_words, w4_scales,
+    tab2_words, tab2_scales, offs2, w8_words, w8_scales, pos1, res, out,
+):
+    nc = tc.nc
+    k_passes, r_passes, n_tiles, col_blocks = K // PASS, H // PASS, N // P, S // COLS
+
+    with ExitStack() as ctx:
+        keep = ctx.enter_context(tc.tile_pool(name="keep", bufs=1))
+        ring = ctx.enter_context(tc.tile_pool(name="ring", bufs=3))
+        psum = ctx.enter_context(tc.psum_pool(name="psum", bufs=1))
+
+        def held(shape, dtype, name):
+            return keep.tile(shape, dtype, name=name, align_bytes=64)
+
+        def bank(number, shape, name):
+            return psum.tile(shape, F32, name=name, tag="bank%d" % number)
+
+        tab_rows = held([P, T], U8, "tab_rows")
+        tab_plane = held([P, T], U8, "tab_plane")
+        tab2_plane = held([P, 1, T3], U8, "tab2_plane")
+        w4_plane = held([P, r_passes, N], U8, "w4_plane")
+        w8_plane = held([P, 1, N], U8, "w8_plane")
+        for plane in (tab_plane, w4_plane, tab2_plane, w8_plane):
+            nc.vector.memset(plane[:].bitcast(I32), 0)
+        for q in range(QUADS):
+            live = slice(32 * q, 32 * q + 4 * k_passes)
+            nc.sync.dma_start(
+                out=tab_rows[live, :].bitcast(I32), in_=tab_scales.bitcast(I32)[:, 4 * q : 4 * q + 4, :]
+            )
+            nc.vector.tensor_copy(out=tab_plane[live, :].bitcast(I32), in_=tab_rows[live, :].bitcast(I32))
+
+        def load_plane(plane, scales):
+            for q in range(QUADS):
+                nc.sync.dma_start(
+                    out=plane[32 * q : 32 * q + 4].bitcast(I32),
+                    in_=scales.bitcast(I32)[:, 4 * q : 4 * q + 4, :].rearrange("a r n -> r a n"),
+                )
+
+        def load_words(tile, words):
+            nc.sync.dma_start(out=tile[:].bitcast(I32), in_=words.rearrange("p t i -> p (t i)").bitcast(I32))
+
+        def load_w1(b, a):
+            raw = held([P, PACK, PASS], F32, "w1_raw%d%d" % (b, a))
+            rows = w1[PASS * a : PASS * (a + 1), PASS * b : PASS * (b + 1)]
+            nc.sync.dma_start(out=raw[:], in_=rows.rearrange("(p j) c -> p j c", j=PACK))
+            return raw
+
+        def load_stain(b, half):
+            tile = held([P, PACK, 2 * COLS], F32, "stain%d%d" % (b, half))
+            rows = stain[PASS * b : PASS * (b + 1), 2 * COLS * half : 2 * COLS * (half + 1)]
+            nc.sync.dma_start(out=tile[:], in_=rows.rearrange("(p t) j -> p t j", t=PACK))
+            return tile
+
+        crop_list = keep.tile([P, S // LIST_ROWS], U16, name="crop_list")
+        strip_list = keep.tile([P, J // LIST_ROWS], U16, name="strip_list")
+        pick_list = keep.tile([P, J // LIST_ROWS], U16, name="pick_list")
+        tab = [held([P, T], U32, "tab%d" % a) for a in range(k_passes)]
+        tab2 = held([P, T3], U32, "tab2")
+        gains = held([P, r_passes, PACK], F32, "gains")
+        w4 = held([P, r_passes, 2 * N], U8, "w4")
+        w8 = held([P, N], U32, "w8")
+        residual = held([P, n_tiles, J], F32, "residual")
+        w1_raw, stains = {}, {}
+
+        nc.sync.dma_start(crop_list[:], offs)
+        load_words(tab[0], tab_words[0])
+        load_words(tab[1], tab_words[1])
+        w1_raw[0, 0] = load_w1(0, 0)
+        w1_raw[0, 1] = load_w1(0, 1)
+        stains[0, 0] = load_stain(0, 0)
+        nc.sync.dma_start(out=gains[:], in_=gain.rearrange("(b p t) -> p b t", p=P, t=PACK))
+        w1_raw[1, 0] = load_w1(1, 0)
+        stains[0, 1] = load_stain(0, 1)
+        w1_raw[1, 1] = load_w1(1, 1)
+        stains[1, 0] = load_stain(1, 0)
+        nc.sync.dma_start(out=w4[:].bitcast(I32), in_=w4_words.bitcast(I32).rearrange("a p n -> p a n"))
+        load_plane(w4_plane, w4_scales)
+        stains[1, 1] = load_stain(1, 1)
+        nc.sync.dma_start(strip_list[:], offs2)
+        load_plane(tab2_plane, tab2_scales)
+        load_words(tab2, tab2_words[0])
+        load_plane(w8_plane, w8_scales)
+        load_words(w8, w8_words[0])
+        nc.sync.dma_start(pick_list[:], pos1)
+        nc.sync.dma_start(out=residual[:], in_=res.rearrange("(c p) j -> p c j", p=P))
+
+        crops = [held([P, S], U32, "crops%d" % a) for a in range(k_passes)]
+        crop_plane = held([P, S], U8, "crop_plane")
+        nc.vector.tensor_copy(crops[0][:], tab[0][:].indirect(crop_list[:]))
+        nc.vector.tensor_copy(crop_plane[:], tab_plane[:].indirect(crop_list[:]))
+        nc.vector.tensor_copy(crops[1][:], tab[1][:].indirect(crop_list[:]))
+
+        w1_lined, w1_codes, w1_planes = {}, {}, {}
+
+        def line_up_w1(b, a, pair, copy):
+            lined = held([P, 2, P, PACK], BF16, "w1_lined%d%d%d" % (b, a, pair))
+            source = w1_raw[b, a][:].rearrange("p j (m t) -> p m j t", t=PACK)[:, :, :, 2 * pair : 2 * pair + 2]
+            copy(out=lined[:].rearrange("p t m j -> p m j t"), in_=source)
+            w1_lined[b, a, pair] = lined
+
+        def quantize_w1(b, a, pair):
+            codes = held([P, 2 * P], U32, "w1_codes%d%d%d" % (b, a, pair))
+            plane = held([P, 2 * P], U8, "w1_plane%d%d%d" % (b, a, pair))
+            nc.vector.quantize_mx(
+                out=codes[:].bitcast(FP8X4),
+                scales=plane[:],
+                in_=w1_lined[b, a, pair][:].rearrange("p t m j -> p (t m j)"),
+            )
+            w1_codes[b, a, pair], w1_planes[b, a, pair] = codes, plane
+
+        for a in range(k_passes):
+            line_up_w1(0, a, 0, nc.vector.tensor_copy)
+            line_up_w1(0, a, 1, nc.scalar.copy)
+            quantize_w1(0, a, 0)
+            quantize_w1(0, a, 1)
+
+        units = [(b, c) for b in range(r_passes) for c in range(col_blocks)]
+        z_tiles, tanh_tiles, h_lined, h_codes, h_planes = {}, {}, {}, {}, {}
+        scores = [held([P, S], F32, "scores%d" % nt) for nt in range(n_tiles)]
+
+        def first_product(u, pair):
+            b, c = units[u]
+            cols = slice(COLS * c, COLS * (c + 1))
+            sums = bank((2 * u + pair) % 4, [P, 2, COLS], "sums%d%d" % (u, pair))
+            for a in range(k_passes):
+                for t in range(2):
+                    rows = slice(P * t, P * (t + 1))
+                    nc.tensor.matmul_mx(
+                        out=sums[:, t, :],
+                        lhsT=w1_codes[b, a, pair][:, rows].bitcast(FP8X4),
+                        lhsT_scale=w1_planes[b, a, pair][:, rows],
+                        rhs=crops[a][:, cols].bitcast(FP8X4),
+                        rhs_scale=crop_plane[4 * a : P, cols],
+                        start=(a == 0 and t == 0),
+                        stop=(a == k_passes - 1 and t == 1),
+                    )
+            if pair == 0:
+                z_tiles[u] = ring.tile([P, PACK, COLS], F32, name="z%d" % u, tag="z")
+            own = slice(COLS * (c % 2), COLS * (c % 2 + 1))
+            nc.vector.tensor_tensor(
+                out=z_tiles[u][:, 2 * pair : 2 * pair + 2, :],
+                in0=sums[:],
+                in1=stains[b, c // 2][:, 2 * pair : 2 * pair + 2, own],
+                op=ADD,
+            )
+
+        def activate(u):
+            tanh_tiles[u] = ring.tile([P, COLS, PACK], F32, name="tanh%d" % u, tag="tanh")
+            nc.scalar.activation(
+                out=tanh_tiles[u][:].rearrange("p (c i) t -> p c t i", i=4),
+                in_=z_tiles[u][:].rearrange("p t (c i) -> p c t i", i=4),
+                func=TANH,
+            )
+
+        def apply_gain(u):
+            b = units[u][0]
+            h_lined[u] = ring.tile([P, COLS, PACK], BF16, name="h_lined%d" % u, tag="h_lined", align_bytes=64)
+            nc.vector.tensor_tensor(
+                out=h_lined[u][:],
+                in0=tanh_tiles[u][:],
+                in1=gains[:, b : b + 1, :].to_broadcast([P, COLS, PACK]),
+                op=MULT,
+            )
+
+        def quantize_h(u):
+            h_codes[u] = held([P, COLS], U32, "h_codes%d" % u)
+            h_planes[u] = held([P, COLS], U8, "h_plane%d" % u)
+            nc.vector.quantize_mx(
+                out=h_codes[u][:].bitcast(FP8X4),
+                scales=h_planes[u][:],
+                in_=h_lined[u][:].rearrange("p j t -> p (j t)"),
+            )
+
+        def second_product(c):
+            for pair in range(2):
+                sums = bank(4 + (2 * c + pair) % 4, [P, 2, COLS], "y_sums%d%d" % (c, pair))
+                for b in range(r_passes):
+                    u = b * col_blocks + c
+                    for i in range(2):
+                        nt = 2 * pair + i
+                        nc.tensor.matmul_mx(
+                            out=sums[:, i, :],
+                            lhsT=w4[:, b, 2 * P * nt : 2 * P * (nt + 1)].bitcast(FP4X4),
+                            lhsT_scale=w4_plane[:, b, P * nt : P * (nt + 1)],
+                            rhs=h_codes[u][:].bitcast(FP8X4),
+                            rhs_scale=h_planes[u][:],
+                            start=(b == 0 and i == 0),
+                            stop=(b == r_passes - 1 and i == 1),
+                        )
+                for i in range(2):
+                    nc.scalar.copy(out=scores[2 * pair + i][:, COLS * c : COLS * (c + 1)], in_=sums[:, i, :])
+
+        def finish(u):
+            quantize_h(u)
+            if units[u][0] == r_passes - 1:
+                second_product(units[u][1])
+
+        for u in range(len(units)):
+            first_product(u, 0)
+            if u >= 2:
+                finish(u - 2)
+            first_product(u, 1)
+            if u in (1, 3):
+                for pair in range(2):
+                    line_up_w1(1, u // 2, pair, nc.scalar.copy)
+                    quantize_w1(1, u // 2, pair)
+            activate(u)
+            if u >= 1:
+                apply_gain(u - 1)
+
+        last = len(units) - 1
+        strips = held([P, J], U32, "strips")
+        strip_plane = held([P, J], U8, "strip_plane")
+        nc.vector.tensor_copy(strips[:], tab2[:].indirect(strip_list[:]))
+        finish(last - 1)
+        apply_gain(last)
+        nc.vector.tensor_copy(strip_plane[:], tab2_plane[:, 0, :].indirect(strip_list[:]))
+        finish(last)
+
+        strip_scores = []
+        for nt in range(n_tiles):
+            sums = bank(nt, [P, J], "strip_scores%d" % nt)
+            nc.tensor.matmul_mx(
+                out=sums[:],
+                lhsT=w8[:, P * nt : P * (nt + 1)].bitcast(FP8X4),
+                lhsT_scale=w8_plane[:, 0, P * nt : P * (nt + 1)],
+                rhs=strips[:].bitcast(FP8X4),
+                rhs_scale=strip_plane[:],
+                start=True,
+                stop=True,
+            )
+            strip_scores.append(sums)
+
+        picked = {}
+
+        def pick(nt):
+            picked[nt] = ring.tile([P, J], F32, name="picked%d" % nt, tag="picked")
+            nc.vector.tensor_tensor(
+                out=picked[nt][:], in0=scores[nt][:].indirect(pick_list[:]), in1=residual[:, nt, :], op=ADD
+            )
+
+        def multiply_and_store(nt):
+            result = held([P, J], F32, "result%d" % nt)
+            nc.vector.tensor_tensor(out=result[:], in0=strip_scores[nt][:], in1=picked[nt][:], op=MULT)
+            nc.sync.dma_start(out=out[P * nt : P * (nt + 1), :], in_=result[:])
+
+        pick(0)
+        for nt in range(1, n_tiles):
+            pick(nt)
+            multiply_and_store(nt - 1)
+        multiply_and_store(n_tiles - 1)

@@ -50,11 +50,14 @@ def tile_list_smear_strip_scores_kernel(
         w8_plane = held([P, 1, N], U8, "w8_plane")
         for plane in (tab_plane, w4_plane, tab2_plane, w8_plane):
             nc.vector.memset(plane[:].bitcast(I32), 0)
-        for q in range(QUADS):
+
+        def load_tab_rows(q):
+            for a in range(k_passes):
+                nc.sync.dma_start(
+                    out=tab_rows[32 * q + 4 * a : 32 * q + 4 * a + 4, :].bitcast(I32),
+                    in_=tab_scales.bitcast(I32)[a, 4 * q : 4 * q + 4, :],
+                )
             live = slice(32 * q, 32 * q + 4 * k_passes)
-            nc.sync.dma_start(
-                out=tab_rows[live, :].bitcast(I32), in_=tab_scales.bitcast(I32)[:, 4 * q : 4 * q + 4, :]
-            )
             nc.vector.tensor_copy(out=tab_plane[live, :].bitcast(I32), in_=tab_rows[live, :].bitcast(I32))
 
         def load_plane(plane, scales):
@@ -73,11 +76,12 @@ def tile_list_smear_strip_scores_kernel(
             nc.sync.dma_start(out=raw[:], in_=rows.rearrange("(p j) c -> p j c", j=PACK))
             return raw
 
-        def load_stain(b, half):
-            tile = held([P, PACK, 2 * COLS], F32, "stain%d%d" % (b, half))
-            rows = stain[PASS * b : PASS * (b + 1), 2 * COLS * half : 2 * COLS * (half + 1)]
+        def load_stain(b, first, blocks):
+            tile = held([P, PACK, blocks * COLS], F32, "stain%d%d" % (b, first))
+            rows = stain[PASS * b : PASS * (b + 1), COLS * first : COLS * (first + blocks)]
             nc.sync.dma_start(out=tile[:], in_=rows.rearrange("(p t) j -> p t j", t=PACK))
-            return tile
+            for i in range(blocks):
+                stains[b, first + i] = tile[:, :, COLS * i : COLS * (i + 1)]
 
         crop_list = keep.tile([P, S // LIST_ROWS], U16, name="crop_list")
         strip_list = keep.tile([P, J // LIST_ROWS], U16, name="strip_list")
@@ -90,20 +94,25 @@ def tile_list_smear_strip_scores_kernel(
         residual = held([P, n_tiles, J], F32, "residual")
         w1_raw, stains = {}, {}
 
+        for q in range(QUADS - 1):
+            load_tab_rows(q)
         nc.sync.dma_start(crop_list[:], offs)
         load_words(tab[0], tab_words[0])
+        load_tab_rows(QUADS - 1)
         load_words(tab[1], tab_words[1])
+        nc.sync.dma_start(out=gains[:], in_=gain.rearrange("(b p t) -> p b t", p=P, t=PACK))
         w1_raw[0, 0] = load_w1(0, 0)
         w1_raw[0, 1] = load_w1(0, 1)
-        stains[0, 0] = load_stain(0, 0)
-        nc.sync.dma_start(out=gains[:], in_=gain.rearrange("(b p t) -> p b t", p=P, t=PACK))
+        load_stain(0, 0, 1)
+        load_stain(0, 1, 1)
         w1_raw[1, 0] = load_w1(1, 0)
-        stains[0, 1] = load_stain(0, 1)
         w1_raw[1, 1] = load_w1(1, 1)
-        stains[1, 0] = load_stain(1, 0)
+        load_stain(0, 2, 1)
+        load_stain(0, 3, 1)
         nc.sync.dma_start(out=w4[:].bitcast(I32), in_=w4_words.bitcast(I32).rearrange("a p n -> p a n"))
+        load_stain(1, 0, 2)
         load_plane(w4_plane, w4_scales)
-        stains[1, 1] = load_stain(1, 1)
+        load_stain(1, 2, 2)
         nc.sync.dma_start(strip_list[:], offs2)
         load_plane(tab2_plane, tab2_scales)
         load_words(tab2, tab2_words[0])
@@ -118,10 +127,16 @@ def tile_list_smear_strip_scores_kernel(
         nc.vector.tensor_copy(crop_plane[:], tab_plane[:].indirect(crop_list[:]))
         nc.vector.tensor_copy(crops[1][:], tab[1][:].indirect(crop_list[:]))
 
+        gain_rows = [held([P, COLS, PACK], F32, "gain_rows%d" % b) for b in range(r_passes)]
+        for b in range(r_passes):
+            nc.scalar.copy(out=gain_rows[b][:], in_=gains[:, b : b + 1, :].to_broadcast([P, COLS, PACK]))
+
         w1_lined, w1_codes, w1_planes = {}, {}, {}
 
         def line_up_w1(b, a, pair, copy):
-            lined = held([P, 2, P, PACK], BF16, "w1_lined%d%d%d" % (b, a, pair))
+            lined = ring.tile(
+                [P, 2, P, PACK], BF16, name="w1_lined%d%d%d" % (b, a, pair), tag="w1_lined", bufs=4, align_bytes=64
+            )
             source = w1_raw[b, a][:].rearrange("p j (m t) -> p m j t", t=PACK)[:, :, :, 2 * pair : 2 * pair + 2]
             copy(out=lined[:].rearrange("p t m j -> p m j t"), in_=source)
             w1_lined[b, a, pair] = lined
@@ -164,11 +179,10 @@ def tile_list_smear_strip_scores_kernel(
                     )
             if pair == 0:
                 z_tiles[u] = ring.tile([P, PACK, COLS], F32, name="z%d" % u, tag="z")
-            own = slice(COLS * (c % 2), COLS * (c % 2 + 1))
             nc.vector.tensor_tensor(
                 out=z_tiles[u][:, 2 * pair : 2 * pair + 2, :],
                 in0=sums[:],
-                in1=stains[b, c // 2][:, 2 * pair : 2 * pair + 2, own],
+                in1=stains[b, c][:, 2 * pair : 2 * pair + 2, :],
                 op=ADD,
             )
 
@@ -186,7 +200,7 @@ def tile_list_smear_strip_scores_kernel(
             nc.vector.tensor_tensor(
                 out=h_lined[u][:],
                 in0=tanh_tiles[u][:],
-                in1=gains[:, b : b + 1, :].to_broadcast([P, COLS, PACK]),
+                in1=gain_rows[b][:],
                 op=MULT,
             )
 
@@ -228,13 +242,13 @@ def tile_list_smear_strip_scores_kernel(
             if u >= 2:
                 finish(u - 2)
             first_product(u, 1)
-            if u in (1, 3):
-                for pair in range(2):
-                    line_up_w1(1, u // 2, pair, nc.scalar.copy)
-                    quantize_w1(1, u // 2, pair)
             activate(u)
+            if u < col_blocks:
+                line_up_w1(1, u % 2, u // 2, nc.scalar.copy)
             if u >= 1:
                 apply_gain(u - 1)
+            if u < col_blocks:
+                quantize_w1(1, u % 2, u // 2)
 
         last = len(units) - 1
         strips = held([P, J], U32, "strips")
@@ -242,8 +256,8 @@ def tile_list_smear_strip_scores_kernel(
         nc.vector.tensor_copy(strips[:], tab2[:].indirect(strip_list[:]))
         finish(last - 1)
         apply_gain(last)
-        nc.vector.tensor_copy(strip_plane[:], tab2_plane[:, 0, :].indirect(strip_list[:]))
         finish(last)
+        nc.vector.tensor_copy(strip_plane[:], tab2_plane[:, 0, :].indirect(strip_list[:]))
 
         strip_scores = []
         for nt in range(n_tiles):

@@ -109,8 +109,8 @@ def tile_list_smear_strip_scores_kernel(
         w1_raw[1, 1] = load_w1(1, 1)
         load_stain(0, 2, 1)
         load_stain(0, 3, 1)
-        nc.sync.dma_start(out=w4[:].bitcast(I32), in_=w4_words.bitcast(I32).rearrange("a p n -> p a n"))
         load_stain(1, 0, 2)
+        nc.sync.dma_start(out=w4[:].bitcast(I32), in_=w4_words.bitcast(I32).rearrange("a p n -> p a n"))
         load_plane(w4_plane, w4_scales)
         load_stain(1, 2, 2)
         nc.sync.dma_start(strip_list[:], offs2)
@@ -178,19 +178,19 @@ def tile_list_smear_strip_scores_kernel(
                         stop=(a == k_passes - 1 and t == 1),
                     )
             if pair == 0:
-                z_tiles[u] = ring.tile([P, PACK, COLS], F32, name="z%d" % u, tag="z")
+                z_tiles[u] = ring.tile([P, 2, COLS, 2], F32, name="z%d" % u, tag="z")
             nc.vector.tensor_tensor(
-                out=z_tiles[u][:, 2 * pair : 2 * pair + 2, :],
-                in0=sums[:],
-                in1=stains[b, c][:, 2 * pair : 2 * pair + 2, :],
+                out=z_tiles[u][:, pair, :, :].rearrange("p (c i) t -> p c t i", i=2),
+                in0=sums[:].rearrange("p t (c i) -> p c t i", i=2),
+                in1=stains[b, c][:, 2 * pair : 2 * pair + 2, :].rearrange("p t (c i) -> p c t i", i=2),
                 op=ADD,
             )
 
         def activate(u):
             tanh_tiles[u] = ring.tile([P, COLS, PACK], F32, name="tanh%d" % u, tag="tanh")
             nc.scalar.activation(
-                out=tanh_tiles[u][:].rearrange("p (c i) t -> p c t i", i=4),
-                in_=z_tiles[u][:].rearrange("p t (c i) -> p c t i", i=4),
+                out=tanh_tiles[u][:].rearrange("p j (pair t) -> p j pair t", t=2),
+                in_=z_tiles[u][:].rearrange("p pair j t -> p j pair t"),
                 func=TANH,
             )
 
@@ -237,18 +237,19 @@ def tile_list_smear_strip_scores_kernel(
             if units[u][0] == r_passes - 1:
                 second_product(units[u][1])
 
+        late_w1 = {1: ((0, 0), (1, 0)), 2: ((0, 1),), 3: ((1, 1),)}
         for u in range(len(units)):
             first_product(u, 0)
             if u >= 2:
                 finish(u - 2)
             first_product(u, 1)
             activate(u)
-            if u < col_blocks:
-                line_up_w1(1, u % 2, u // 2, nc.scalar.copy)
+            for a, pair in late_w1.get(u, ()):
+                line_up_w1(1, a, pair, nc.scalar.copy)
             if u >= 1:
                 apply_gain(u - 1)
-            if u < col_blocks:
-                quantize_w1(1, u % 2, u // 2)
+            for a, pair in late_w1.get(u, ()):
+                quantize_w1(1, a, pair)
 
         last = len(units) - 1
         strips = held([P, J], U32, "strips")

@@ -23,6 +23,7 @@ PASS = P * PACK
 QUADS = 4
 COLS = 256
 LIST_ROWS = 16
+GAIN_COLS = 32
 
 
 def tile_list_smear_strip_scores_kernel(
@@ -51,14 +52,12 @@ def tile_list_smear_strip_scores_kernel(
         for plane in (tab_plane, w4_plane, tab2_plane, w8_plane):
             nc.vector.memset(plane[:].bitcast(I32), 0)
 
-        def load_tab_rows(q):
+        def load_tab_rows(q, tile):
             for a in range(k_passes):
                 nc.sync.dma_start(
-                    out=tab_rows[32 * q + 4 * a : 32 * q + 4 * a + 4, :].bitcast(I32),
+                    out=tile[32 * q + 4 * a : 32 * q + 4 * a + 4, :].bitcast(I32),
                     in_=tab_scales.bitcast(I32)[a, 4 * q : 4 * q + 4, :],
                 )
-            live = slice(32 * q, 32 * q + 4 * k_passes)
-            nc.vector.tensor_copy(out=tab_plane[live, :].bitcast(I32), in_=tab_rows[live, :].bitcast(I32))
 
         def load_plane(plane, scales):
             for q in range(QUADS):
@@ -95,15 +94,17 @@ def tile_list_smear_strip_scores_kernel(
         w1_raw, stains = {}, {}
 
         for q in range(QUADS - 1):
-            load_tab_rows(q)
-        nc.sync.dma_start(crop_list[:], offs)
+            load_tab_rows(q, tab_rows)
+            live = slice(32 * q, 32 * q + 4 * k_passes)
+            nc.vector.tensor_copy(out=tab_plane[live, :].bitcast(I32), in_=tab_rows[live, :].bitcast(I32))
         load_words(tab[0], tab_words[0])
-        load_tab_rows(QUADS - 1)
+        nc.sync.dma_start(crop_list[:], offs)
+        load_tab_rows(QUADS - 1, tab_plane)
         load_words(tab[1], tab_words[1])
-        nc.sync.dma_start(out=gains[:], in_=gain.rearrange("(b p t) -> p b t", p=P, t=PACK))
         w1_raw[0, 0] = load_w1(0, 0)
         w1_raw[0, 1] = load_w1(0, 1)
         load_stain(0, 0, 1)
+        nc.sync.dma_start(out=gains[:], in_=gain.rearrange("(b p t) -> p b t", p=P, t=PACK))
         load_stain(0, 1, 1)
         w1_raw[1, 0] = load_w1(1, 0)
         w1_raw[1, 1] = load_w1(1, 1)
@@ -126,10 +127,6 @@ def tile_list_smear_strip_scores_kernel(
         nc.vector.tensor_copy(crops[0][:], tab[0][:].indirect(crop_list[:]))
         nc.vector.tensor_copy(crop_plane[:], tab_plane[:].indirect(crop_list[:]))
         nc.vector.tensor_copy(crops[1][:], tab[1][:].indirect(crop_list[:]))
-
-        gain_rows = [held([P, COLS, PACK], F32, "gain_rows%d" % b) for b in range(r_passes)]
-        for b in range(r_passes):
-            nc.scalar.copy(out=gain_rows[b][:], in_=gains[:, b : b + 1, :].to_broadcast([P, COLS, PACK]))
 
         w1_lined, w1_codes, w1_planes = {}, {}, {}
 
@@ -156,6 +153,10 @@ def tile_list_smear_strip_scores_kernel(
             line_up_w1(0, a, 1, nc.scalar.copy)
             quantize_w1(0, a, 0)
             quantize_w1(0, a, 1)
+
+        gain_rows = held([P, r_passes, GAIN_COLS, PACK], F32, "gain_rows")
+        for b in range(r_passes):
+            nc.scalar.copy(out=gain_rows[:, b, :, :], in_=gains[:, b : b + 1, :].to_broadcast([P, GAIN_COLS, PACK]))
 
         units = [(b, c) for b in range(r_passes) for c in range(col_blocks)]
         z_tiles, tanh_tiles, h_lined, h_codes, h_planes = {}, {}, {}, {}, {}
@@ -198,9 +199,11 @@ def tile_list_smear_strip_scores_kernel(
             b = units[u][0]
             h_lined[u] = ring.tile([P, COLS, PACK], BF16, name="h_lined%d" % u, tag="h_lined", align_bytes=64)
             nc.vector.tensor_tensor(
-                out=h_lined[u][:],
-                in0=tanh_tiles[u][:],
-                in1=gain_rows[b][:],
+                out=h_lined[u][:].rearrange("p (g j) t -> p g (j t)", j=GAIN_COLS),
+                in0=tanh_tiles[u][:].rearrange("p (g j) t -> p g (j t)", j=GAIN_COLS),
+                in1=gain_rows[:, b : b + 1, :, :]
+                .rearrange("p b j t -> p b (j t)")
+                .to_broadcast([P, COLS // GAIN_COLS, GAIN_COLS * PACK]),
                 op=MULT,
             )
 
@@ -212,6 +215,8 @@ def tile_list_smear_strip_scores_kernel(
                 scales=h_planes[u][:],
                 in_=h_lined[u][:].rearrange("p j t -> p (j t)"),
             )
+
+        y_sums = {}
 
         def second_product(c):
             for pair in range(2):
@@ -229,8 +234,13 @@ def tile_list_smear_strip_scores_kernel(
                             start=(b == 0 and i == 0),
                             stop=(b == r_passes - 1 and i == 1),
                         )
-                for i in range(2):
-                    nc.scalar.copy(out=scores[2 * pair + i][:, COLS * c : COLS * (c + 1)], in_=sums[:, i, :])
+                y_sums[c, pair] = sums
+
+        def copy_scores(u):
+            b, c = units[u]
+            if b == r_passes - 1:
+                for nt in range(n_tiles):
+                    nc.scalar.copy(out=scores[nt][:, COLS * c : COLS * (c + 1)], in_=y_sums[c, nt // 2][:, nt % 2, :])
 
         def finish(u):
             quantize_h(u)
@@ -244,6 +254,8 @@ def tile_list_smear_strip_scores_kernel(
                 finish(u - 2)
             first_product(u, 1)
             activate(u)
+            if u >= 2:
+                copy_scores(u - 2)
             for a, pair in late_w1.get(u, ()):
                 line_up_w1(1, a, pair, nc.scalar.copy)
             if u >= 1:
@@ -256,8 +268,10 @@ def tile_list_smear_strip_scores_kernel(
         strip_plane = held([P, J], U8, "strip_plane")
         nc.vector.tensor_copy(strips[:], tab2[:].indirect(strip_list[:]))
         finish(last - 1)
+        copy_scores(last - 1)
         apply_gain(last)
         finish(last)
+        copy_scores(last)
         nc.vector.tensor_copy(strip_plane[:], tab2_plane[:, 0, :].indirect(strip_list[:]))
 
         strip_scores = []
@@ -282,13 +296,16 @@ def tile_list_smear_strip_scores_kernel(
                 out=picked[nt][:], in0=scores[nt][:].indirect(pick_list[:]), in1=residual[:, nt, :], op=ADD
             )
 
-        def multiply_and_store(nt):
-            result = held([P, J], F32, "result%d" % nt)
-            nc.vector.tensor_tensor(out=result[:], in0=strip_scores[nt][:], in1=picked[nt][:], op=MULT)
-            nc.sync.dma_start(out=out[P * nt : P * (nt + 1), :], in_=result[:])
+        def multiply_and_store(nt, parts=1):
+            width = J // parts
+            for part in range(parts):
+                cols = slice(width * part, width * (part + 1))
+                result = held([P, width], F32, "result%d%d" % (nt, part))
+                nc.vector.tensor_tensor(out=result[:], in0=strip_scores[nt][:, cols], in1=picked[nt][:, cols], op=MULT)
+                nc.sync.dma_start(out=out[P * nt : P * (nt + 1), cols], in_=result[:])
 
         pick(0)
         for nt in range(1, n_tiles):
             pick(nt)
             multiply_and_store(nt - 1)
-        multiply_and_store(n_tiles - 1)
+        multiply_and_store(n_tiles - 1, parts=2)

from contextlib import ExitStack

import concourse.mybir as mybir

K, H, M, N, T, S, T3, J = 1024, 1024, 512, 512, 4096, 1024, 2048, 512
FLOPS = 2 * (K * H * S + H * N * S + M * N * J)

F32 = mybir.dt.float32
BF16 = mybir.dt.bfloat16
I32 = mybir.dt.int32
U32 = mybir.dt.uint32
U16 = mybir.dt.uint16
U8 = mybir.dt.uint8
FP8X4 = mybir.dt.float8_e4m3fn_x4
FP4X4 = mybir.dt.float4_e2m1fn_x4
ADD = mybir.AluOpType.add
MULT = mybir.AluOpType.mult
TANH = mybir.ActivationFunctionType.Tanh

P = 128
PACK = 4
PASS = P * PACK
QUADS = 4
COLS = 256
LIST_ROWS = 16
GAIN_COLS = 32


def tile_list_smear_strip_scores_kernel(
    tc, tab_words, tab_scales, offs, w1, stain, gain, w4_words, w4_scales,
    tab2_words, tab2_scales, offs2, w8_words, w8_scales, pos1, res, out,
):
    nc = tc.nc
    k_passes, r_passes, n_tiles, col_blocks = K // PASS, H // PASS, N // P, S // COLS

    with ExitStack() as ctx:
        keep = ctx.enter_context(tc.tile_pool(name="keep", bufs=1))
        ring = ctx.enter_context(tc.tile_pool(name="ring", bufs=3))
        psum = ctx.enter_context(tc.psum_pool(name="psum", bufs=1))

        def held(shape, dtype, name):
            return keep.tile(shape, dtype, name=name, align_bytes=64)

        def bank(number, shape, name):
            return psum.tile(shape, F32, name=name, tag="bank%d" % number)

        tab_rows = held([P, T], U8, "tab_rows")
        tab_plane = held([P, T], U8, "tab_plane")
        tab2_plane = held([P, 1, T3], U8, "tab2_plane")
        w4_plane = held([P, r_passes, N], U8, "w4_plane")
        w8_plane = held([P, 1, N], U8, "w8_plane")
        for plane in (tab_plane, w4_plane, tab2_plane, w8_plane):
            nc.vector.memset(plane[:].bitcast(I32), 0)

        def load_tab_rows(q, tile):
            for a in range(k_passes):
                nc.sync.dma_start(
                    out=tile[32 * q + 4 * a : 32 * q + 4 * a + 4, :].bitcast(I32),
                    in_=tab_scales.bitcast(I32)[a, 4 * q : 4 * q + 4, :],
                )

        def load_plane(plane, scales):
            for q in range(QUADS):
                nc.sync.dma_start(
                    out=plane[32 * q : 32 * q + 4].bitcast(I32),
                    in_=scales.bitcast(I32)[:, 4 * q : 4 * q + 4, :].rearrange("a r n -> r a n"),
                )

        def load_words(tile, words):
            nc.sync.dma_start(out=tile[:].bitcast(I32), in_=words.rearrange("p t i -> p (t i)").bitcast(I32))

        def load_w1(b, a):
            raw = held([P, PACK, PASS], F32, "w1_raw%d%d" % (b, a))
            rows = w1[PASS * a : PASS * (a + 1), PASS * b : PASS * (b + 1)]
            nc.sync.dma_start(out=raw[:], in_=rows.rearrange("(p j) c -> p j c", j=PACK))
            return raw

        def load_stain(b, first, blocks):
            tile = held([P, PACK, blocks * COLS], F32, "stain%d%d" % (b, first))
            rows = stain[PASS * b : PASS * (b + 1), COLS * first : COLS * (first + blocks)]
            nc.sync.dma_start(out=tile[:], in_=rows.rearrange("(p t) j -> p t j", t=PACK))
            for i in range(blocks):
                stains[b, first + i] = tile[:, :, COLS * i : COLS * (i + 1)]

        crop_list = keep.tile([P, S // LIST_ROWS], U16, name="crop_list")
        strip_list = keep.tile([P, J // LIST_ROWS], U16, name="strip_list")
        pick_list = keep.tile([P, J // LIST_ROWS], U16, name="pick_list")
        tab = [held([P, T], U32, "tab%d" % a) for a in range(k_passes)]
        tab2 = held([P, T3], U32, "tab2")
        gains = held([P, r_passes, PACK], F32, "gains")
        w4 = held([P, r_passes, 2 * N], U8, "w4")
        w8 = held([P, N], U32, "w8")
        residual = held([P, n_tiles, J], F32, "residual")
        w1_raw, stains = {}, {}

        for q in range(QUADS - 1):
            load_tab_rows(q, tab_rows)
            live = slice(32 * q, 32 * q + 4 * k_passes)
            nc.vector.tensor_copy(out=tab_plane[live, :].bitcast(I32), in_=tab_rows[live, :].bitcast(I32))
        load_words(tab[0], tab_words[0])
        nc.sync.dma_start(crop_list[:], offs)
        load_tab_rows(QUADS - 1, tab_plane)
        load_words(tab[1], tab_words[1])
        w1_raw[0, 0] = load_w1(0, 0)
        w1_raw[0, 1] = load_w1(0, 1)
        load_stain(0, 0, 1)
        nc.sync.dma_start(out=gains[:], in_=gain.rearrange("(b p t) -> p b t", p=P, t=PACK))
        load_stain(0, 1, 1)
        w1_raw[1, 0] = load_w1(1, 0)
        w1_raw[1, 1] = load_w1(1, 1)
        load_stain(0, 2, 1)
        load_stain(0, 3, 1)
        load_stain(1, 0, 2)
        nc.sync.dma_start(out=w4[:].bitcast(I32), in_=w4_words.bitcast(I32).rearrange("a p n -> p a n"))
        load_plane(w4_plane, w4_scales)
        load_stain(1, 2, 2)
        nc.sync.dma_start(strip_list[:], offs2)
        load_plane(tab2_plane, tab2_scales)
        load_words(tab2, tab2_words[0])
        load_plane(w8_plane, w8_scales)
        load_words(w8, w8_words[0])
        nc.sync.dma_start(pick_list[:], pos1)
        nc.sync.dma_start(out=residual[:], in_=res.rearrange("(c p) j -> p c j", p=P))

        crops = [held([P, S], U32, "crops%d" % a) for a in range(k_passes)]
        crop_plane = held([P, S], U8, "crop_plane")
        nc.vector.tensor_copy(crops[0][:], tab[0][:].indirect(crop_list[:]))
        nc.vector.tensor_copy(crop_plane[:], tab_plane[:].indirect(crop_list[:]))
        nc.vector.tensor_copy(crops[1][:], tab[1][:].indirect(crop_list[:]))

        w1_lined, w1_codes, w1_planes = {}, {}, {}

        def line_up_w1(b, a, pair, copy):
            lined = ring.tile(
                [P, 2, P, PACK], BF16, name="w1_lined%d%d%d" % (b, a, pair), tag="w1_lined", bufs=4, align_bytes=64
            )
            source = w1_raw[b, a][:].rearrange("p j (m t) -> p m j t", t=PACK)[:, :, :, 2 * pair : 2 * pair + 2]
            copy(out=lined[:].rearrange("p t m j -> p m j t"), in_=source)
            w1_lined[b, a, pair] = lined

        def quantize_w1(b, a, pair):
            codes = held([P, 2 * P], U32, "w1_codes%d%d%d" % (b, a, pair))
            plane = held([P, 2 * P], U8, "w1_plane%d%d%d" % (b, a, pair))
            nc.vector.quantize_mx(
                out=codes[:].bitcast(FP8X4),
                scales=plane[:],
                in_=w1_lined[b, a, pair][:].rearrange("p t m j -> p (t m j)"),
            )
            w1_codes[b, a, pair], w1_planes[b, a, pair] = codes, plane

        for a in range(k_passes):
            line_up_w1(0, a, 0, nc.vector.tensor_copy)
            line_up_w1(0, a, 1, nc.scalar.copy)
            quantize_w1(0, a, 0)
            quantize_w1(0, a, 1)

        gain_rows = held([P, r_passes, GAIN_COLS, PACK], F32, "gain_rows")
        for b in range(r_passes):
            nc.scalar.copy(out=gain_rows[:, b, :, :], in_=gains[:, b : b + 1, :].to_broadcast([P, GAIN_COLS, PACK]))

        units = [(b, c) for b in range(r_passes) for c in range(col_blocks)]
        z_tiles, tanh_tiles, h_lined, h_codes, h_planes = {}, {}, {}, {}, {}
        scores = [held([P, S], F32, "scores%d" % nt) for nt in range(n_tiles)]

        def first_product(u, pair):
            b, c = units[u]
            cols = slice(COLS * c, COLS * (c + 1))
            sums = bank((2 * u + pair) % 4, [P, 2, COLS], "sums%d%d" % (u, pair))
            for a in range(k_passes):
                for t in range(2):
                    rows = slice(P * t, P * (t + 1))
                    nc.tensor.matmul_mx(
                        out=sums[:, t, :],
                        lhsT=w1_codes[b, a, pair][:, rows].bitcast(FP8X4),
                        lhsT_scale=w1_planes[b, a, pair][:, rows],
                        rhs=crops[a][:, cols].bitcast(FP8X4),
                        rhs_scale=crop_plane[4 * a : P, cols],
                        start=(a == 0 and t == 0),
                        stop=(a == k_passes - 1 and t == 1),
                    )
            if pair == 0:
                z_tiles[u] = ring.tile([P, 2, COLS, 2], F32, name="z%d" % u, tag="z")
            nc.vector.tensor_tensor(
                out=z_tiles[u][:, pair, :, :].rearrange("p (c i) t -> p c t i", i=2),
                in0=sums[:].rearrange("p t (c i) -> p c t i", i=2),
                in1=stains[b, c][:, 2 * pair : 2 * pair + 2, :].rearrange("p t (c i) -> p c t i", i=2),
                op=ADD,
            )

        def activate(u):
            tanh_tiles[u] = ring.tile([P, COLS, PACK], F32, name="tanh%d" % u, tag="tanh")
            nc.scalar.activation(
                out=tanh_tiles[u][:].rearrange("p j (pair t) -> p j pair t", t=2),
                in_=z_tiles[u][:].rearrange("p pair j t -> p j pair t"),
                func=TANH,
            )

        def apply_gain(u):
            b = units[u][0]
            h_lined[u] = ring.tile([P, COLS, PACK], BF16, name="h_lined%d" % u, tag="h_lined", align_bytes=64)
            nc.vector.tensor_tensor(
                out=h_lined[u][:].rearrange("p (g j) t -> p g (j t)", j=GAIN_COLS),
                in0=tanh_tiles[u][:].rearrange("p (g j) t -> p g (j t)", j=GAIN_COLS),
                in1=gain_rows[:, b : b + 1, :, :]
                .rearrange("p b j t -> p b (j t)")
                .to_broadcast([P, COLS // GAIN_COLS, GAIN_COLS * PACK]),
                op=MULT,
            )

        def quantize_h(u):
            h_codes[u] = held([P, COLS], U32, "h_codes%d" % u)
            h_planes[u] = held([P, COLS], U8, "h_plane%d" % u)
            nc.vector.quantize_mx(
                out=h_codes[u][:].bitcast(FP8X4),
                scales=h_planes[u][:],
                in_=h_lined[u][:].rearrange("p j t -> p (j t)"),
            )

        y_sums = {}

        def second_product(c):
            for pair in range(2):
                sums = bank(4 + (2 * c + pair) % 4, [P, 2, COLS], "y_sums%d%d" % (c, pair))
                for b in range(r_passes):
                    u = b * col_blocks + c
                    for i in range(2):
                        nt = 2 * pair + i
                        nc.tensor.matmul_mx(
                            out=sums[:, i, :],
                            lhsT=w4[:, b, 2 * P * nt : 2 * P * (nt + 1)].bitcast(FP4X4),
                            lhsT_scale=w4_plane[:, b, P * nt : P * (nt + 1)],
                            rhs=h_codes[u][:].bitcast(FP8X4),
                            rhs_scale=h_planes[u][:],
                            start=(b == 0 and i == 0),
                            stop=(b == r_passes - 1 and i == 1),
                        )
                y_sums[c, pair] = sums

        def copy_scores(u):
            b, c = units[u]
            if b == r_passes - 1:
                for nt in range(n_tiles):
                    nc.scalar.copy(out=scores[nt][:, COLS * c : COLS * (c + 1)], in_=y_sums[c, nt // 2][:, nt % 2, :])

        def finish(u):
            quantize_h(u)
            if units[u][0] == r_passes - 1:
                second_product(units[u][1])

        late_w1 = {1: ((0, 0), (1, 0)), 2: ((0, 1),), 3: ((1, 1),)}
        for u in range(len(units)):
            first_product(u, 0)
            if u >= 2:
                finish(u - 2)
            first_product(u, 1)
            activate(u)
            if u >= 2:
                copy_scores(u - 2)
            for a, pair in late_w1.get(u, ()):
                line_up_w1(1, a, pair, nc.scalar.copy)
            if u >= 1:
                apply_gain(u - 1)
            for a, pair in late_w1.get(u, ()):
                quantize_w1(1, a, pair)

        last = len(units) - 1
        strips = held([P, J], U32, "strips")
        strip_plane = held([P, J], U8, "strip_plane")
        nc.vector.tensor_copy(strips[:], tab2[:].indirect(strip_list[:]))
        finish(last - 1)
        copy_scores(last - 1)
        apply_gain(last)
        finish(last)
        copy_scores(last)
        nc.vector.tensor_copy(strip_plane[:], tab2_plane[:, 0, :].indirect(strip_list[:]))

        strip_scores = []
        for nt in range(n_tiles):
            sums = bank(nt, [P, J], "strip_scores%d" % nt)
            nc.tensor.matmul_mx(
                out=sums[:],
                lhsT=w8[:, P * nt : P * (nt + 1)].bitcast(FP8X4),
                lhsT_scale=w8_plane[:, 0, P * nt : P * (nt + 1)],
                rhs=strips[:].bitcast(FP8X4),
                rhs_scale=strip_plane[:],
                start=True,
                stop=True,
            )
            strip_scores.append(sums)

        picked = {}

        def pick(nt):
            picked[nt] = ring.tile([P, J], F32, name="picked%d" % nt, tag="picked")
            nc.vector.tensor_tensor(
                out=picked[nt][:], in0=scores[nt][:].indirect(pick_list[:]), in1=residual[:, nt, :], op=ADD
            )

        def multiply_and_store(nt, parts=1):
            width = J // parts
            for part in range(parts):
                cols = slice(width * part, width * (part + 1))
                result = held([P, width], F32, "result%d%d" % (nt, part))
                nc.vector.tensor_tensor(out=result[:], in0=strip_scores[nt][:, cols], in1=picked[nt][:, cols], op=MULT)
                nc.sync.dma_start(out=out[P * nt : P * (nt + 1), cols], in_=result[:])

        pick(0)
        for nt in range(1, n_tiles):
            pick(nt)
            multiply_and_store(nt - 1)
        multiply_and_store(n_tiles - 1, parts=2)
